import numpy as np, ml_dtypes
CORES = [1,14,19,24,37,42,55,60,65,78,83,88,101,106,119,124]
N = 16
TK, LAY = 128, 4
def setup_inputs(rng):
    return {"x": rng.standard_normal((N, 128, TK), dtype=np.float32).astype(ml_dtypes.bfloat16), "wu": (rng.standard_normal((N, 128, LAY * 256), dtype=np.float32) / 16).astype(ml_dtypes.bfloat16), "wd": (rng.standard_normal((N, 128, 256), dtype=np.float32) / 16).astype(ml_dtypes.bfloat16)}
def setup_inputs_big(rng):
    d = setup_inputs(rng)
    for k in ("x",): d[k] = (d[k].astype(np.float32) * 1048576.0).astype(d[k].dtype)
    return d
def setup_inputs_small(rng):
    d = setup_inputs(rng)
    for k in ("x",): d[k] = (d[k].astype(np.float32) * (1 / 1048576.0)).astype(d[k].dtype)
    return d
def setup_inputs_apart(rng):
    d = setup_inputs(rng)
    f = (10.0 ** rng.permutation(np.linspace(-1.5, 1.5, N))).astype(np.float32).reshape(N, 1, 1)
    for k in ("x",): d[k] = (d[k].astype(np.float32) * f).astype(d[k].dtype)
    return d
def reference(x, wu, wd):
    X, WU, WD = x.astype(np.float64), wu.astype(np.float64), wd.astype(np.float64)
    s = list(X)
    for l in range(LAY):
        for q in range(0, N, 2 << l):
            p = q + (1 << l)
            s[q] = np.maximum(WU[q][:, 256 * l:256 * l + 128].T @ s[q] + WU[q][:, 256 * l + 128:256 * l + 256].T @ s[p], 0.0)
    for l in range(LAY - 1, -1, -1):
        for q in range(0, N, 2 << l):
            p = q + (1 << l)
            s[p] = np.maximum(WD[p][:, 0:128].T @ s[p] + WD[p][:, 128:256].T @ s[q], 0.0)
    return {"y": np.stack(s).astype(ml_dtypes.bfloat16)}

@@ -1,0 +1,268 @@
+from concourse.bass import DstId, RemoteDMATransfer
+from concourse.mybir import AluOpType
+
+N, LAY, TK = 16, 4, 128
+SPAN = 4
+NBANK = 8
+NLD, NAR, NND = 4, 20, 14
+
+
+def _tz(p):
+    k = 0
+    while not (p >> k) & 1:
+        k += 1
+    return k
+
+
+def _levels(q):
+    return LAY if q == 0 else _tz(q)
+
+
+def _parent(p):
+    return p & (p - 1)
+
+
+def _pre(r, l):
+    return ("x", r) if l == 0 else ("up", r, l - 1)
+
+
+def _final(r):
+    return ("dn", r) if r else ("up", 0, LAY - 1)
+
+
+def _ops(nd):
+    if nd[0] == "up":
+        q, l = nd[1], nd[2]
+        return ("wu", q, l), _pre(q, l), _pre(q + (1 << l), l)
+    p = nd[1]
+    return ("wd", p), _pre(p, _tz(p)), _final(_parent(p))
+
+
+def _when(v):
+    if v[0] in ("x", "wu", "wd"):
+        return 0
+    if v[0] == "up":
+        return 2 if v[2] == 0 else 3 + v[2]
+    return _when(_final(_parent(v[1]))) + (2 if v[1] % 2 else 1)
+
+
+def _layout():
+    off, pos = {}, 0
+    for r in range(N):
+        blocks = [(("x", r), TK)]
+        blocks += [(("wu", r, l), 2 * TK) for l in range(_levels(r))]
+        blocks += [(("wd", r), 2 * TK)] if r else []
+        for v, w in blocks:
+            off[v] = (pos, pos + w)
+            pos += w
+    for l in range(LAY):
+        for q in range(0, N, 2 << l):
+            off[("up", q, l)] = (pos, pos + TK)
+            pos += TK
+    for p in range(1, N):
+        off[("dn", p)] = (pos, pos + TK)
+        pos += TK
+    return off, pos
+
+
+OFF, COLS = _layout()
+
+SCRATCH = {"m": ("sbuf", [128, COLS], "bfloat16"), "zero": ("sbuf", [128, TK], "float32")}
+for _b in range(NBANK):
+    SCRATCH["ps%d" % _b] = ("psum", [128, 512], "float32")
+SEMAPHORES = (["ld%d" % i for i in range(NLD)] + ["ar%d" % i for i in range(NAR)] + ["mm%d" % i for i in range(NND)]
+              + ["vv%d" % i for i in range(NND)] + ["z", "st", "sent"])
+
+_CACHE = {}
+
+
+def _plan(topo, cores):
+    if "p" in _CACHE:
+        return _CACHE["p"]
+
+    def ok(a, b):
+        return a == b or topo.may_write(cores[a], cores[b])
+
+    free = [r for r in range(N) if all(ok(r, s) for s in range(N))]
+    top = {}
+    for b in range(0, N, SPAN):
+        t = [c for c in range(b, b + SPAN) if c in free and all(ok(s, c) for s in range(0, N, 2))][0]
+        for r in range(b, b + SPAN):
+            top[r] = t
+    tops = sorted(set(top.values()))
+    place = {}
+
+    def put(nd, r):
+        if r not in place.setdefault(nd, []):
+            place[nd].append(r)
+
+    for q in range(0, N, 2):
+        cand = [top[q]] + sorted(free, key=lambda c: abs(c - q))
+        put(("up", q, 0), [c for c in cand if ok(q, c) and ok(q + 1, c)][0])
+    for t in tops:
+        for l in range(1, LAY):
+            for q in range(0, N, 2 << l):
+                put(("up", q, l), t)
+    for r in range(N):
+        if r % 2:
+            put(("dn", r), r)
+        p = r - r % 2
+        while p:
+            put(("dn", p), top[r])
+            p = _parent(p)
+
+    need = {}
+    for nd, where in place.items():
+        for r in where:
+            for v in _ops(nd):
+                need.setdefault(v, set()).add(r)
+    for r in range(N):
+        need.setdefault(_final(r), set()).add(r)
+
+    sends = {}
+    for v, readers in need.items():
+        makers = place[v] if v in place else [v[1]]
+        for d in sorted(readers):
+            if d not in makers:
+                s = makers[0] if len(makers) == 1 else top[d]
+                sends.setdefault(s, {}).setdefault(v, []).append(d)
+
+    msgs = {r: [] for r in range(N)}
+    used = {r: set() for r in range(N)}
+    for s in sorted(sends):
+        items = []
+        for v, ds in sends[s].items():
+            late = [d for d in ds if _final(d) == v and len(ds) > 1]
+            items.append((_when(v), OFF[v][0], v, [d for d in ds if d not in late]))
+            if late:
+                items.append((_when(v) + 1.5, OFF[v][0], v, late))
+        items = [(it[2], it[3]) for it in sorted(items)]
+        merged = []
+        for v, ds in items:
+            if merged and merged[-1][1] == ds and OFF[merged[-1][0][-1]][1] == OFF[v][0] and _when(v) == 0:
+                merged[-1][0].append(v)
+            else:
+                merged.append(([v], ds))
+        for vs, ds in merged:
+            ds = sorted(ds, key=lambda d: (-sum(d in place[nd] for nd in place if nd[0] == "dn"), (d - s) % N))
+            k = 0
+            while any(k in used[d] for d in ds):
+                k += 1
+            for d in ds:
+                used[d].add(k)
+            msgs[s].append((vs, ds, k))
+    _CACHE["p"] = (place, need, msgs)
+    return _CACHE["p"]
+
+
+def _engines(topo, cores, s, ds):
+    mask = topo.mask(cores[s], cores[ds[0]])
+    for d in ds[1:]:
+        mask &= topo.mask(cores[s], cores[d])
+    return mask, bin(mask).count("1")
+
+
+def rank_program(g, core, T, topo):
+    r = T.rank_of(core)
+    if r is None:
+        return
+    cores = list(T.cores)
+    place, need, msgs = _plan(topo, cores)
+    m = T.m
+    ev = {}
+
+    def blk(v):
+        return m[:, OFF[v][0]:OFF[v][1]]
+
+    waited = set()
+
+    def wait(name, queue, v):
+        s, n = ev[v]
+        if (name, s) not in waited:
+            waited.add((name, s))
+            queue.wait_ge(T.sem[s], n)
+
+    for s in range(N):
+        for vs, ds, k in msgs[s]:
+            if r in ds:
+                for v in vs:
+                    ev[v] = ("ar%d" % k, _engines(topo, cores, s, ds)[1])
+
+    mine = [v for v in need if v[0] in ("x", "wu", "wd") and v[1] == r]
+    pieces = [[v for v in mine if v[0] == "x"], [v for v in mine if v[0] == "wu" and v[2] == 0],
+              sorted(v for v in mine if v[0] == "wu" and v[2] > 0), [v for v in mine if v[0] == "wd"]]
+    pieces = [p for p in pieces if p]
+    for i, p in enumerate(pieces):
+        queue = (g.sync, g.scalar)[i % 2]
+        lo, hi = OFF[p[0]][0], OFF[p[-1]][1]
+        if p[0][0] == "wu":
+            src = T.wu[:, 2 * TK * p[0][2]:2 * TK * (p[-1][2] + 1)]
+        else:
+            src = (T.x if p[0][0] == "x" else T.wd)[:, :]
+        queue.dma_start(m[:, lo:hi], src).then_inc(T.sem["ld%d" % i], 16)
+        for v in p:
+            ev[v] = ("ld%d" % i, 16)
+
+    halves = []
+    for nd in place:
+        if r in place[nd]:
+            t = _when(nd)
+            halves.append((t - 0.5 if nd[0] == "dn" else t, OFF[nd][0], 0, nd))
+            halves.append((t, OFF[nd][0], 1, nd))
+    halves.sort()
+    order, begun = [], set()
+    for h in halves:
+        if h[3] in begun:
+            order.append(h[3])
+        begun.add(h[3])
+    for i, nd in enumerate(order):
+        ev[nd] = ("vv%d" % i, 1)
+
+    bank, last = {}, {}
+    for _, _, part, nd in halves:
+        w, a, b = _ops(nd)
+        first = nd not in bank
+        if first:
+            spare = [k for k in range(NBANK) if k not in last]
+            if spare:
+                bank[nd] = spare[0]
+            else:
+                bank[nd] = min(last, key=lambda k: order.index(last[k]))
+                wait("tensor", g.tensor, last[bank[nd]])
+            last[bank[nd]] = nd
+        wait("tensor", g.tensor, w)
+        wait("tensor", g.tensor, (a, b)[part])
+        c = OFF[w][0] + part * TK
+        ins = g.tensor.matmul(T["ps%d" % bank[nd]][:, 0:TK], m[:, c:c + TK], blk((a, b)[part]), first, not first)
+        if not first:
+            ins.then_inc(T.sem["mm%d" % order.index(nd)], 1)
+
+    if order:
+        g.vector.memset(T.zero[:, :], 0.0).then_inc(T.sem.z, 1)
+        g.vector.wait_ge(T.sem.z, 1)
+    for i, nd in enumerate(order):
+        g.vector.wait_ge(T.sem["mm%d" % i], 1)
+        g.vector.tensor_tensor(blk(nd), T["ps%d" % bank[nd]][:, 0:TK], T.zero[:, :], AluOpType.max).then_inc(
+            T.sem["vv%d" % i], 1)
+
+    sent = 0
+    for vs, ds, k in msgs[r]:
+        for v in vs:
+            wait("g", g, v)
+        mask, n = _engines(topo, cores, r, ds)
+        ap = m[:, OFF[vs[0]][0]:OFF[vs[-1]][1]]
+        ids = [topo.addr(cores[d]) for d in ds]
+        if len(ds) == 1:
+            g.remote_dma(out_ap=ap, in_ap=ap, remote_sem=T.sem["ar%d" % k], local_sem=T.sem.sent, pid=ids[0][1],
+                         routing_id=ids[0][0], dma_engine_mask=mask)
+        else:
+            g.remote_dma_fused([RemoteDMATransfer(dst_ids=[DstId(rid=a[0], pnc=a[1]) for a in ids],
+                                                  dma_engine_mask=mask, remote_sem=T.sem["ar%d" % k], srcs=[ap],
+                                                  dsts=[ap for _ in ds], alu_op=0)], local_sem=T.sem.sent)
+        sent += n
+    if sent:
+        g.wait_ge(T.sem.sent, sent)
+
+    wait("sync", g.sync, _final(r))
+    g.sync.dma_start(T.y[:, :], blk(_final(r))).then_inc(T.sem.st, 16)
+    g.sync.wait_ge(T.sem.st, 16)

@@ -2,9 +2,9 @@ from concourse.bass import DstId, RemoteDMATransfer
 from concourse.mybir import AluOpType
 
 N, LAY, TK = 16, 4, 128
-SPAN = 4
-NBANK = 8
-NLD, NAR, NND = 4, 20, 14
+NSIM = 128
+NQ = N // 4
+NLD, NAR, NND = 4, 12, 6
 
 
 def _tz(p):
@@ -38,14 +38,6 @@ def _ops(nd):
     return ("wd", p), _pre(p, _tz(p)), _final(_parent(p))
 
 
-def _when(v):
-    if v[0] in ("x", "wu", "wd"):
-        return 0
-    if v[0] == "up":
-        return 2 if v[2] == 0 else 3 + v[2]
-    return _when(_final(_parent(v[1]))) + (2 if v[1] % 2 else 1)
-
-
 def _layout():
     off, pos = {}, 0
     for r in range(N):
@@ -68,7 +60,7 @@ def _layout():
 OFF, COLS = _layout()
 
 SCRATCH = {"m": ("sbuf", [128, COLS], "bfloat16"), "zero": ("sbuf", [128, TK], "float32")}
-for _b in range(NBANK):
+for _b in range(NND):
     SCRATCH["ps%d" % _b] = ("psum", [128, 512], "float32")
 SEMAPHORES = (["ld%d" % i for i in range(NLD)] + ["ar%d" % i for i in range(NAR)] + ["mm%d" % i for i in range(NND)]
               + ["vv%d" % i for i in range(NND)] + ["z", "st", "sent"])
@@ -76,98 +68,112 @@ SEMAPHORES = (["ld%d" % i for i in range(NLD)] + ["ar%d" % i for i in range(NAR)
 _CACHE = {}
 
 
-def _plan(topo, cores):
+def _plan(topo, ranks):
     if "p" in _CACHE:
         return _CACHE["p"]
+    cores, taken = list(ranks), set(ranks)
 
-    def ok(a, b):
-        return a == b or topo.may_write(cores[a], cores[b])
+    def pick(near, targets):
+        cand = [c for c in range(NSIM) if topo.chip(c) == topo.chip(near) and c not in taken
+                and all(topo.may_write(c, t) for t in targets)]
+        cand.sort(key=lambda c: (topo.die(c) != topo.die(near), c))
+        taken.add(cand[0])
+        cores.append(cand[0])
 
-    free = [r for r in range(N) if all(ok(r, s) for s in range(N))]
-    top = {}
-    for b in range(0, N, SPAN):
-        t = [c for c in range(b, b + SPAN) if c in free and all(ok(s, c) for s in range(0, N, 2))][0]
-        for r in range(b, b + SPAN):
-            top[r] = t
-    tops = sorted(set(top.values()))
-    place = {}
+    for k in range(NQ):
+        pick(ranks[4 * k], ranks)
+    for k in range(NQ):
+        pick(ranks[4 * k + 3], [ranks[4 * k]])
+    P = [N + k for k in range(NQ)]
+    R = [N + NQ + k for k in range(NQ)]
+    H = N // 2
 
-    def put(nd, r):
-        if r not in place.setdefault(nd, []):
-            place[nd].append(r)
-
-    for q in range(0, N, 2):
-        cand = [top[q]] + sorted(free, key=lambda c: abs(c - q))
-        put(("up", q, 0), [c for c in cand if ok(q, c) and ok(q + 1, c)][0])
-    for t in tops:
-        for l in range(1, LAY):
-            for q in range(0, N, 2 << l):
-                put(("up", q, l), t)
-    for r in range(N):
-        if r % 2:
-            put(("dn", r), r)
-        p = r - r % 2
+    work = {s: [] for s in range(len(cores))}
+    e, f, t = ("up", H, LAY - 2), ("up", 0, LAY - 2), ("up", 0, LAY - 1)
+    for k in range(NQ):
+        q = 4 * k
+        for nd in (("up", q, 0), ("up", q + 2, 0), ("up", q, 1)):
+            work[q] += [(nd, 0), (nd, 1)]
+        for r in (q + 1, q + 3):
+            work[r] = [(("dn", r), 0), (("dn", r), 1)]
+        path, p = [("dn", q + 2)], q
         while p:
-            put(("dn", p), top[r])
+            path.insert(0, ("dn", p))
             p = _parent(p)
+        early = [nd for nd in path if _ops(nd)[1] not in (e, f, t)] + [nd for nd in path if _ops(nd)[1] in (e, f, t)]
+        work[P[k]] = ([(e, 0), (e, 1), (f, 0), (f, 1)] + [(nd, 0) for nd in early] + [(t, 1), (t, 0)]
+                      + [(nd, 1) for nd in path])
 
-    need = {}
-    for nd, where in place.items():
-        for r in where:
-            for v in _ops(nd):
-                need.setdefault(v, set()).add(r)
-    for r in range(N):
-        need.setdefault(_final(r), set()).add(r)
+    msgs = {s: [] for s in range(len(cores))}
+    used = {s: set() for s in range(len(cores))}
 
-    sends = {}
-    for v, readers in need.items():
-        makers = place[v] if v in place else [v[1]]
-        for d in sorted(readers):
-            if d not in makers:
-                s = makers[0] if len(makers) == 1 else top[d]
-                sends.setdefault(s, {}).setdefault(v, []).append(d)
+    def send(s, vs, ds, wide=False):
+        for d in ds:
+            if not topo.may_write(cores[s], cores[d]):
+                raise ValueError("site %d may not write to site %d" % (s, d))
+        k = 0
+        while any(k in used[d] for d in ds):
+            k += 1
+        for d in ds:
+            used[d].add(k)
+        msgs[s].append((vs, ds, k, wide))
 
-    msgs = {r: [] for r in range(N)}
-    used = {r: set() for r in range(N)}
-    for s in sorted(sends):
-        items = []
-        for v, ds in sends[s].items():
-            late = [d for d in ds if _final(d) == v and len(ds) > 1]
-            items.append((_when(v), OFF[v][0], v, [d for d in ds if d not in late]))
-            if late:
-                items.append((_when(v) + 1.5, OFF[v][0], v, late))
-        items = [(it[2], it[3]) for it in sorted(items)]
-        merged = []
-        for v, ds in items:
-            if merged and merged[-1][1] == ds and OFF[merged[-1][0][-1]][1] == OFF[v][0] and _when(v) == 0:
-                merged[-1][0].append(v)
-            else:
-                merged.append(([v], ds))
-        for vs, ds in merged:
-            ds = sorted(ds, key=lambda d: (-sum(d in place[nd] for nd in place if nd[0] == "dn"), (d - s) % N))
-            k = 0
-            while any(k in used[d] for d in ds):
-                k += 1
-            for d in ds:
-                used[d].add(k)
-            msgs[s].append((vs, ds, k))
-    _CACHE["p"] = (place, need, msgs)
+    def spread(s, vs, ds):
+        far = [d for d in ds if topo.chip(cores[d]) != topo.chip(cores[s])]
+        near = [d for d in ds if d not in far]
+        if far:
+            send(s, vs, far)
+        if near:
+            send(s, vs, near)
+
+    for l in range(2, LAY):
+        spread(0, [("wu", 0, l)], [P[1], P[0]])
+        send(P[1], [("wu", 0, l)], [P[3]])
+        send(P[0], [("wu", 0, l)], [P[2]])
+    spread(H, [("wu", H, 2)], [P[3], P[2]])
+    send(P[3], [("wu", H, 2)], [P[1]])
+    send(P[2], [("wu", H, 2)], [P[0]])
+    spread(H, [("wd", H)], [P[3], P[2]])
+    for k in range(NQ):
+        q = 4 * k
+        if q and q != H:
+            send(q, [("wd", q)], [P[k]], True)
+        send(q + 1, [("x", q + 1)], [q])
+        send(q + 2, [("x", q + 2), ("wu", q + 2, 0)], [q])
+        send(q + 2, [("wd", q + 2)], [P[k]])
+        send(q + 3, [("x", q + 3)], [R[k]])
+        send(R[k], [("x", q + 3)], [q])
+    for k in range(NQ):
+        q = 4 * k
+        spread(q, [("up", q, 1)], [P[j] for j in range(NQ - 1, -1, -1)])
+        send(q, [("up", q + 2, 0)], [P[k]])
+    for k in range(NQ):
+        q = 4 * k
+        send(P[k], [_final(q)], [q + 1])
+        send(P[k], [_final(q + 2)], [q + 3, q + 2])
+        send(P[k], [_final(q)], [q])
+    _CACHE["p"] = (cores, work, msgs)
     return _CACHE["p"]
 
 
-def _engines(topo, cores, s, ds):
+def _engines(topo, cores, s, ds, wide):
     mask = topo.mask(cores[s], cores[ds[0]])
     for d in ds[1:]:
         mask &= topo.mask(cores[s], cores[d])
+    far = mask
+    for c in cores:
+        if c != cores[s]:
+            far &= topo.mask(cores[s], c)
+    if not wide and mask & ~far:
+        mask &= ~far
     return mask, bin(mask).count("1")
 
 
 def rank_program(g, core, T, topo):
-    r = T.rank_of(core)
-    if r is None:
+    cores, work, msgs = _plan(topo, list(T.cores))
+    if core not in cores:
         return
-    cores = list(T.cores)
-    place, need, msgs = _plan(topo, cores)
+    me = cores.index(core)
     m = T.m
     ev = {}
 
@@ -182,74 +188,63 @@ def rank_program(g, core, T, topo):
             waited.add((name, s))
             queue.wait_ge(T.sem[s], n)
 
-    for s in range(N):
-        for vs, ds, k in msgs[s]:
-            if r in ds:
+    for s in range(len(cores)):
+        for vs, ds, k, wide in msgs[s]:
+            if me in ds:
                 for v in vs:
-                    ev[v] = ("ar%d" % k, _engines(topo, cores, s, ds)[1])
+                    ev[v] = ("ar%d" % k, _engines(topo, cores, s, ds, wide)[1])
 
-    mine = [v for v in need if v[0] in ("x", "wu", "wd") and v[1] == r]
-    pieces = [[v for v in mine if v[0] == "x"], [v for v in mine if v[0] == "wu" and v[2] == 0],
-              sorted(v for v in mine if v[0] == "wu" and v[2] > 0), [v for v in mine if v[0] == "wd"]]
-    pieces = [p for p in pieces if p]
-    for i, p in enumerate(pieces):
-        queue = (g.sync, g.scalar)[i % 2]
-        lo, hi = OFF[p[0]][0], OFF[p[-1]][1]
-        if p[0][0] == "wu":
-            src = T.wu[:, 2 * TK * p[0][2]:2 * TK * (p[-1][2] + 1)]
-        else:
-            src = (T.x if p[0][0] == "x" else T.wd)[:, :]
-        queue.dma_start(m[:, lo:hi], src).then_inc(T.sem["ld%d" % i], 16)
-        for v in p:
-            ev[v] = ("ld%d" % i, 16)
+    if me < N:
+        lv = _levels(me)
+        top = [[("wu", me, l)] for l in range(2, lv)]
+        wd = [[("wd", me)]] if me else []
+        low = [[("wu", me, l) for l in range(min(lv, 2))]] if lv else []
+        pieces = top + wd + [[("x", me)]] + low if top else [[("x", me)]] + low + wd
+        for i, p in enumerate(pieces):
+            queue = (g.sync, g.scalar)[i % 2]
+            lo, hi = OFF[p[0]][0], OFF[p[-1]][1]
+            if p[0][0] == "wu":
+                src = T.wu[:, 2 * TK * p[0][2]:2 * TK * (p[-1][2] + 1)]
+            else:
+                src = (T.x if p[0][0] == "x" else T.wd)[:, :]
+            queue.dma_start(m[:, lo:hi], src).then_inc(T.sem["ld%d" % i], 16)
+            for v in p:
+                ev[v] = ("ld%d" % i, 16)
 
-    halves = []
-    for nd in place:
-        if r in place[nd]:
-            t = _when(nd)
-            halves.append((t - 0.5 if nd[0] == "dn" else t, OFF[nd][0], 0, nd))
-            halves.append((t, OFF[nd][0], 1, nd))
-    halves.sort()
     order, begun = [], set()
-    for h in halves:
-        if h[3] in begun:
-            order.append(h[3])
-        begun.add(h[3])
+    for nd, _ in work[me]:
+        if nd in begun:
+            order.append(nd)
+        begun.add(nd)
     for i, nd in enumerate(order):
         ev[nd] = ("vv%d" % i, 1)
 
-    bank, last = {}, {}
-    for _, _, part, nd in halves:
+    open_ = set()
+    for nd, part in work[me]:
         w, a, b = _ops(nd)
-        first = nd not in bank
-        if first:
-            spare = [k for k in range(NBANK) if k not in last]
-            if spare:
-                bank[nd] = spare[0]
-            else:
-                bank[nd] = min(last, key=lambda k: order.index(last[k]))
-                wait("tensor", g.tensor, last[bank[nd]])
-            last[bank[nd]] = nd
+        first = nd not in open_
+        open_.add(nd)
         wait("tensor", g.tensor, w)
         wait("tensor", g.tensor, (a, b)[part])
         c = OFF[w][0] + part * TK
-        ins = g.tensor.matmul(T["ps%d" % bank[nd]][:, 0:TK], m[:, c:c + TK], blk((a, b)[part]), first, not first)
+        i = order.index(nd)
+        ins = g.tensor.matmul(T["ps%d" % i][:, 0:TK], m[:, c:c + TK], blk((a, b)[part]), first, not first)
         if not first:
-            ins.then_inc(T.sem["mm%d" % order.index(nd)], 1)
+            ins.then_inc(T.sem["mm%d" % i], 1)
 
     if order:
         g.vector.memset(T.zero[:, :], 0.0).then_inc(T.sem.z, 1)
         g.vector.wait_ge(T.sem.z, 1)
     for i, nd in enumerate(order):
         g.vector.wait_ge(T.sem["mm%d" % i], 1)
-        g.vector.tensor_tensor(blk(nd), T["ps%d" % bank[nd]][:, 0:TK], T.zero[:, :], AluOpType.max).then_inc(
+        g.vector.tensor_tensor(blk(nd), T["ps%d" % i][:, 0:TK], T.zero[:, :], AluOpType.max).then_inc(
             T.sem["vv%d" % i], 1)
 
     sent = 0
-    for vs, ds, k in msgs[r]:
+    for vs, ds, k, wide in msgs[me]:
         for v in vs:
             wait("g", g, v)
-        mask, n = _engines(topo, cores, r, ds)
+        mask, n = _engines(topo, cores, me, ds, wide)
         ap = m[:, OFF[vs[0]][0]:OFF[vs[-1]][1]]
         ids = [topo.addr(cores[d]) for d in ds]
         if len(ds) == 1:
@@ -263,6 +258,7 @@ def rank_program(g, core, T, topo):
     if sent:
         g.wait_ge(T.sem.sent, sent)
 
-    wait("sync", g.sync, _final(r))
-    g.sync.dma_start(T.y[:, :], blk(_final(r))).then_inc(T.sem.st, 16)
-    g.sync.wait_ge(T.sem.st, 16)
+    if me < N:
+        wait("sync", g.sync, _final(me))
+        g.sync.dma_start(T.y[:, :], blk(_final(me))).then_inc(T.sem.st, 16)
+        g.sync.wait_ge(T.sem.st, 16)

from concourse.bass import DstId, RemoteDMATransfer
from concourse.mybir import AluOpType

N, LAY, TK = 16, 4, 128
NSIM = 128
NQ = N // 4
NLD, NAR, NND = 4, 12, 6


def _tz(p):
    k = 0
    while not (p >> k) & 1:
        k += 1
    return k


def _levels(q):
    return LAY if q == 0 else _tz(q)


def _parent(p):
    return p & (p - 1)


def _pre(r, l):
    return ("x", r) if l == 0 else ("up", r, l - 1)


def _final(r):
    return ("dn", r) if r else ("up", 0, LAY - 1)


def _ops(nd):
    if nd[0] == "up":
        q, l = nd[1], nd[2]
        return ("wu", q, l), _pre(q, l), _pre(q + (1 << l), l)
    p = nd[1]
    return ("wd", p), _pre(p, _tz(p)), _final(_parent(p))


def _layout():
    off, pos = {}, 0
    for r in range(N):
        blocks = [(("x", r), TK)]
        blocks += [(("wu", r, l), 2 * TK) for l in range(_levels(r))]
        blocks += [(("wd", r), 2 * TK)] if r else []
        for v, w in blocks:
            off[v] = (pos, pos + w)
            pos += w
    for l in range(LAY):
        for q in range(0, N, 2 << l):
            off[("up", q, l)] = (pos, pos + TK)
            pos += TK
    for p in range(1, N):
        off[("dn", p)] = (pos, pos + TK)
        pos += TK
    return off, pos


OFF, COLS = _layout()

SCRATCH = {"m": ("sbuf", [128, COLS], "bfloat16"), "zero": ("sbuf", [128, TK], "float32")}
for _b in range(NND):
    SCRATCH["ps%d" % _b] = ("psum", [128, 512], "float32")
SEMAPHORES = (["ld%d" % i for i in range(NLD)] + ["ar%d" % i for i in range(NAR)] + ["mm%d" % i for i in range(NND)]
              + ["vv%d" % i for i in range(NND)] + ["z", "st", "sent"])

_CACHE = {}


def _plan(topo, ranks):
    if "p" in _CACHE:
        return _CACHE["p"]
    cores, taken = list(ranks), set(ranks)

    def pick(near, targets):
        cand = [c for c in range(NSIM) if topo.chip(c) == topo.chip(near) and c not in taken
                and all(topo.may_write(c, t) for t in targets)]
        cand.sort(key=lambda c: (topo.die(c) != topo.die(near), c))
        taken.add(cand[0])
        cores.append(cand[0])

    for k in range(NQ):
        pick(ranks[4 * k], ranks)
    for k in range(NQ):
        pick(ranks[4 * k + 3], [ranks[4 * k]])
    P = [N + k for k in range(NQ)]
    R = [N + NQ + k for k in range(NQ)]
    H = N // 2

    work = {s: [] for s in range(len(cores))}
    e, f, t = ("up", H, LAY - 2), ("up", 0, LAY - 2), ("up", 0, LAY - 1)
    for k in range(NQ):
        q = 4 * k
        for nd in (("up", q, 0), ("up", q + 2, 0), ("up", q, 1)):
            work[q] += [(nd, 0), (nd, 1)]
        for r in (q + 1, q + 3):
            work[r] = [(("dn", r), 0), (("dn", r), 1)]
        path, p = [("dn", q + 2)], q
        while p:
            path.insert(0, ("dn", p))
            p = _parent(p)
        early = [nd for nd in path if _ops(nd)[1] not in (e, f, t)] + [nd for nd in path if _ops(nd)[1] in (e, f, t)]
        work[P[k]] = ([(e, 0), (e, 1), (f, 0), (f, 1)] + [(nd, 0) for nd in early] + [(t, 1), (t, 0)]
                      + [(nd, 1) for nd in path])

    msgs = {s: [] for s in range(len(cores))}
    used = {s: set() for s in range(len(cores))}

    def send(s, vs, ds, wide=False):
        for d in ds:
            if not topo.may_write(cores[s], cores[d]):
                raise ValueError("site %d may not write to site %d" % (s, d))
        k = 0
        while any(k in used[d] for d in ds):
            k += 1
        for d in ds:
            used[d].add(k)
        msgs[s].append((vs, ds, k, wide))

    def spread(s, vs, ds):
        far = [d for d in ds if topo.chip(cores[d]) != topo.chip(cores[s])]
        near = [d for d in ds if d not in far]
        if far:
            send(s, vs, far)
        if near:
            send(s, vs, near)

    for l in range(2, LAY):
        spread(0, [("wu", 0, l)], [P[1], P[0]])
        send(P[1], [("wu", 0, l)], [P[3]])
        send(P[0], [("wu", 0, l)], [P[2]])
    spread(H, [("wu", H, 2)], [P[3], P[2]])
    send(P[3], [("wu", H, 2)], [P[1]])
    send(P[2], [("wu", H, 2)], [P[0]])
    spread(H, [("wd", H)], [P[3], P[2]])
    for k in range(NQ):
        q = 4 * k
        if q and q != H:
            send(q, [("wd", q)], [P[k]], True)
        send(q + 1, [("x", q + 1)], [q])
        send(q + 2, [("x", q + 2), ("wu", q + 2, 0)], [q])
        send(q + 2, [("wd", q + 2)], [P[k]])
        send(q + 3, [("x", q + 3)], [R[k]])
        send(R[k], [("x", q + 3)], [q])
    for k in range(NQ):
        q = 4 * k
        spread(q, [("up", q, 1)], [P[j] for j in range(NQ - 1, -1, -1)])
        send(q, [("up", q + 2, 0)], [P[k]])
    for k in range(NQ):
        q = 4 * k
        send(P[k], [_final(q)], [q + 1])
        send(P[k], [_final(q + 2)], [q + 3, q + 2])
        send(P[k], [_final(q)], [q])
    _CACHE["p"] = (cores, work, msgs)
    return _CACHE["p"]


def _engines(topo, cores, s, ds, wide):
    mask = topo.mask(cores[s], cores[ds[0]])
    for d in ds[1:]:
        mask &= topo.mask(cores[s], cores[d])
    far = mask
    for c in cores:
        if c != cores[s]:
            far &= topo.mask(cores[s], c)
    if not wide and mask & ~far:
        mask &= ~far
    return mask, bin(mask).count("1")


def rank_program(g, core, T, topo):
    cores, work, msgs = _plan(topo, list(T.cores))
    if core not in cores:
        return
    me = cores.index(core)
    m = T.m
    ev = {}

    def blk(v):
        return m[:, OFF[v][0]:OFF[v][1]]

    waited = set()

    def wait(name, queue, v):
        s, n = ev[v]
        if (name, s) not in waited:
            waited.add((name, s))
            queue.wait_ge(T.sem[s], n)

    for s in range(len(cores)):
        for vs, ds, k, wide in msgs[s]:
            if me in ds:
                for v in vs:
                    ev[v] = ("ar%d" % k, _engines(topo, cores, s, ds, wide)[1])

    if me < N:
        lv = _levels(me)
        top = [[("wu", me, l)] for l in range(2, lv)]
        wd = [[("wd", me)]] if me else []
        low = [[("wu", me, l) for l in range(min(lv, 2))]] if lv else []
        pieces = top + wd + [[("x", me)]] + low if top else [[("x", me)]] + low + wd
        for i, p in enumerate(pieces):
            queue = (g.sync, g.scalar)[i % 2]
            lo, hi = OFF[p[0]][0], OFF[p[-1]][1]
            if p[0][0] == "wu":
                src = T.wu[:, 2 * TK * p[0][2]:2 * TK * (p[-1][2] + 1)]
            else:
                src = (T.x if p[0][0] == "x" else T.wd)[:, :]
            queue.dma_start(m[:, lo:hi], src).then_inc(T.sem["ld%d" % i], 16)
            for v in p:
                ev[v] = ("ld%d" % i, 16)

    order, begun = [], set()
    for nd, _ in work[me]:
        if nd in begun:
            order.append(nd)
        begun.add(nd)
    for i, nd in enumerate(order):
        ev[nd] = ("vv%d" % i, 1)

    open_ = set()
    for nd, part in work[me]:
        w, a, b = _ops(nd)
        first = nd not in open_
        open_.add(nd)
        wait("tensor", g.tensor, w)
        wait("tensor", g.tensor, (a, b)[part])
        c = OFF[w][0] + part * TK
        i = order.index(nd)
        ins = g.tensor.matmul(T["ps%d" % i][:, 0:TK], m[:, c:c + TK], blk((a, b)[part]), first, not first)
        if not first:
            ins.then_inc(T.sem["mm%d" % i], 1)

    if order:
        g.vector.memset(T.zero[:, :], 0.0).then_inc(T.sem.z, 1)
        g.vector.wait_ge(T.sem.z, 1)
    for i, nd in enumerate(order):
        g.vector.wait_ge(T.sem["mm%d" % i], 1)
        g.vector.tensor_tensor(blk(nd), T["ps%d" % i][:, 0:TK], T.zero[:, :], AluOpType.max).then_inc(
            T.sem["vv%d" % i], 1)

    sent = 0
    for vs, ds, k, wide in msgs[me]:
        for v in vs:
            wait("g", g, v)
        mask, n = _engines(topo, cores, me, ds, wide)
        ap = m[:, OFF[vs[0]][0]:OFF[vs[-1]][1]]
        ids = [topo.addr(cores[d]) for d in ds]
        if len(ds) == 1:
            g.remote_dma(out_ap=ap, in_ap=ap, remote_sem=T.sem["ar%d" % k], local_sem=T.sem.sent, pid=ids[0][1],
                         routing_id=ids[0][0], dma_engine_mask=mask)
        else:
            g.remote_dma_fused([RemoteDMATransfer(dst_ids=[DstId(rid=a[0], pnc=a[1]) for a in ids],
                                                  dma_engine_mask=mask, remote_sem=T.sem["ar%d" % k], srcs=[ap],
                                                  dsts=[ap for _ in ds], alu_op=0)], local_sem=T.sem.sent)
        sent += n
    if sent:
        g.wait_ge(T.sem.sent, sent)

    if me < N:
        wait("sync", g.sync, _final(me))
        g.sync.dma_start(T.y[:, :], blk(_final(me))).then_inc(T.sem.st, 16)
        g.sync.wait_ge(T.sem.st, 16)
